import numpy as np
import ml_dtypes


def mxq(x, axis, fmt="e4m3"):
    dtype, down = {"e4m3": (ml_dtypes.float8_e4m3fn, 7), "e5m2": (ml_dtypes.float8_e5m2, 14)}[fmt]
    v = np.moveaxis(np.asarray(x, np.float32).astype(ml_dtypes.bfloat16).astype(np.float64), axis, -1)
    blocks = v.reshape(v.shape[:-1] + (-1, 32))
    amax = np.abs(blocks).max(-1, keepdims=True)
    byte = np.maximum(np.where(amax > 0, np.frexp(amax)[1] - 1 + 127, 0) - down, 1)
    scale = np.exp2(byte - 127.0)
    codes = (blocks / scale).astype(np.float32).astype(dtype).astype(np.float64)
    return np.moveaxis((codes * scale).reshape(v.shape), -1, axis)


WIDE = False


def mx_kscale(k):
    if not WIDE:
        return np.ones(k)
    levels = np.array([10, -10, 5, -5, 0])
    if k % 512:
        return np.exp2(np.random.permutation(np.resize(levels, k // 32))).repeat(32)
    a = np.empty((k // 512, 16))
    for p in range(k // 512):
        a[p, :8] = np.random.permutation(np.resize(levels, 8))
        for g in range(8):
            far = levels[np.abs(levels - a[p, g]) >= 10]
            a[p, g + 8] = far[np.random.randint(len(far))]
    return np.exp2(a.ravel()).repeat(32)


BF16 = ml_dtypes.bfloat16


def bf(x):
    return np.asarray(x, np.float32).astype(BF16)


def f64(x):
    return np.asarray(x).astype(np.float64)


M, K, T, V = 1024, 1024, 2048, 1024


def draw0():
    s = mx_kscale(K)
    v = mx_kscale(T)
    u = mx_kscale(M)
    return {
        "x": bf(np.random.standard_normal((M, K)) * s / u[:, None]),
        "c": bf(np.random.standard_normal((M, T)) * v / u[:, None]),
        "ws": bf(np.random.standard_normal((K, V)) / np.sqrt(K) / s[:, None]),
        "wt": bf(np.random.standard_normal((T, V)) / np.sqrt(T) / v[:, None]),
        "r": bf(np.random.uniform(0.5, 1.5, M) * u * u),
    }


def core(x, c, ws, wt, r):
    zs = mxq(f64(x), 1, "e4m3") @ mxq(f64(ws), 0, "e4m3")
    zt = mxq(f64(c), 1, "e4m3") @ mxq(f64(wt), 0, "e4m3")
    d = (zs - zt) * f64(r)[:, None]
    xt = mxq(f64(x), 0, "e4m3")
    dq = mxq(d, 0, "e4m3")
    g = (xt.T @ dq) / np.sqrt(M)
    return zs, zt, g


def e4m3fn_bytes(y):
    return np.clip(np.asarray(y, np.float64), -448.0, 448.0).astype(np.float32).astype(ml_dtypes.float8_e4m3fn).view(np.uint8)


def e4m3fn_values(b):
    return np.asarray(b, np.uint8).view(ml_dtypes.float8_e4m3fn).astype(np.float64)


def setup_inputs():
    d = draw0()
    x0 = np.asarray(d['wt']).astype(np.float64)
    s = (np.max(np.abs(x0), axis=(1,), keepdims=True) / 448.0).astype(np.float32)
    out = {}
    for k, v in d.items():
        if k == 'wt':
            out['wt_bytes'] = e4m3fn_bytes(x0 / s.astype(np.float64))
            out['wt_scale'] = s
        else:
            out[k] = v
    return out


def reference(x, c, ws, wt_bytes, wt_scale, r):
    return core(x, c, ws, e4m3fn_values(wt_bytes) * wt_scale.astype(np.float64), r)

from contextlib import ExitStack

import concourse.mybir as mybir
from concourse.masks import make_identity

F32 = mybir.dt.float32
BF16 = mybir.dt.bfloat16
U32 = mybir.dt.uint32
U8 = mybir.dt.uint8
FP8 = mybir.dt.float8_e4m3fn
FP8X4 = mybir.dt.float8_e4m3fn_x4
ACT = mybir.ActivationFunctionType
ALU = mybir.AluOpType

P = 128
M, K, T, V = 1024, 1024, 2048, 1024
FLOPS = 2 * M * V * (K + T) + 2 * M * K * V
NC = 256
CH = V // NC

def interleave(dst, src):
    return dict(out=dst.rearrange("p (c i) t -> p c t i", i=4), in_=src.rearrange("p t (c i) -> p c t i", i=4))


def tile_logit_matching_distillation_s7_kernel(tc, x, c, ws, wt_bytes, wt_scale, r, zs_out, zt_out, g_out):
    nc = tc.nc
    with ExitStack() as ctx:
        sb = ctx.enter_context(tc.tile_pool(name="sb", bufs=1))
        ps = ctx.enter_context(tc.psum_pool(name="ps", bufs=1))

        def new(tag, shape, dtype, bufs=1):
            return sb.tile([P] + shape, dtype, tag=tag, name=tag, bufs=bufs, align_bytes=64)

        def bank(tag, shape, bufs):
            return ps.tile([P] + shape, F32, tag=tag, name=tag, bufs=bufs)

        def copy(e, out, in_):
            if e == "S":
                nc.scalar.copy(out=out, in_=in_)
            else:
                nc.vector.tensor_copy(out=out, in_=in_)

        x_v = x.rearrange("(g p t) k -> g p t k", g=2, t=4)
        c_v = c.rearrange("(g p t) k -> g p t k", g=2, t=4)
        ws_v = ws.rearrange("(q p j) v -> q p j v", p=P, j=4)
        wt_v = wt_bytes.rearrange("(q p j) v -> q p j v", p=P, j=4)
        zs_v = zs_out.rearrange("(g p t) v -> g p t v", g=2, t=4)
        zt_v = zt_out.rearrange("(g p t) v -> g p t v", g=2, t=4)
        g_v = g_out.rearrange("(b p) v -> p b v", p=P)

        scale_sb = new("wscale", [4, 4], F32)
        nc.scalar.dma_start(out=scale_sb[:], in_=wt_scale.rearrange("(q p j) o -> p q (j o)", p=P, j=4))
        r_sb = new("r", [2, 4], BF16)
        nc.scalar.dma_start(out=r_sb[:], in_=r.rearrange("(g p t) -> p g t", g=2, t=4))
        x_sb, c_sb, ws_sb, wt_sb = {}, {}, {}, {}
        def load_x(i):
            g, h = divmod(i, 2)
            if h == 0:
                x_sb[g] = new("x_in%d" % g, [4, K], BF16)
            nc.sync.dma_start(out=x_sb[g][:, 2 * h : 2 * h + 2, :], in_=x_v[g][:, 2 * h : 2 * h + 2, :])
        def load_c(i):
            g, h = divmod(i, 2)
            c_sb[i] = new("big%d" % (i % 4), [2, T], BF16)
            nc.sync.dma_start(out=c_sb[i][:], in_=c_v[g][:, 2 * h : 2 * h + 2, :])
        def load_ws(q):
            ws_sb[q] = new("big%d" % (q + 2), [4, V], BF16)
            nc.sync.dma_start(out=ws_sb[q][:], in_=ws_v[q])
        def load_wt(q):
            wt_sb[q] = new("wtb%d" % q, [4, V], U8)
            nc.sync.dma_start(out=wt_sb[q][:], in_=wt_v[q])
        load_x(0); load_ws(0); load_x(1); load_ws(1); load_wt(0); load_x(2); load_c(0); load_wt(1); load_x(3); load_wt(2); load_c(1); load_wt(3)

        ident = new("ident", [P], F32)
        make_identity(nc, ident[:])
        r32 = new("r32", [2, 4], F32)

        tp, tq = {}, {}
        xc, cc, wsc, wtc, xgc, dc = {}, {}, {}, {}, {}, {}
        inter, wide = {}, {}
        zs, zt, d0, dI, acc, gs = {}, {}, {}, {}, {}, {}

        def T_x(i):
            for k in range(2):
                b = tp["x", i, k] = bank("tp", [4, P], 4)
                words = x_sb[i // 2][:, 2 * (i % 2) + k, :].bitcast(F32)
                for q in range(2):
                    for u in range(2):
                        nc.tensor.transpose(b[:, 2 * q + u, :], words[:, 256 * q + u : 256 * (q + 1) : 2], ident[:])

        def evac(e, b, dst):
            copy(e, dst.bitcast(F32).rearrange("p (q m u) -> p q m u", q=2, u=2), b[:].rearrange("p (q u) m -> p q m u", u=2))

        def E_x(i, k, e):
            if k == 0:
                tq["x", i] = new("tq", [2048], BF16, 4)
            evac(e, tp["x", i, k], tq["x", i][:, 1024 * k : 1024 * (k + 1)])

        def quant(tag, src, n, bufs=1):
            codes, planes = new("c_" + tag, [n // 4], U32, bufs), new("s_" + tag, [n // 4], U8, bufs)
            nc.vector.quantize_mx(out=codes[:].bitcast(FP8X4), scales=planes[:], in_=src)
            return codes, planes

        def Q_x(i):
            xc[i] = quant("x%d" % i, tq["x", i][:], 2048)

        def WSI(q, h, e="V"):
            inter["ws", q, h] = new("inter", [512, 4], BF16, 3)
            copy(e, **interleave(inter["ws", q, h][:], ws_sb[q][:, :, 512 * h : 512 * (h + 1)]))

        def flat(t):
            return t[:].rearrange("p n t -> p (n t)")

        def WSQ(q, h):
            wsc[q, h] = quant("wa%d" % (2 * q + h), flat(inter["ws", q, h]), 2048)

        def MZs(i, k, h):
            b = acc["zs", i, k, h] = bank("acc", [512], 4)
            xcod, xpl = xc[i]
            for q in range(2):
                m = slice((2 * k + q) * P, (2 * k + q + 1) * P)
                w, wp = wsc[q, h]
                nc.tensor.matmul_mx(out=b[:], lhsT=xcod[:, m].bitcast(FP8X4), lhsT_scale=xpl[:, m], rhs=w[:].bitcast(FP8X4), rhs_scale=wp[:], start=q == 0, stop=q == 1)

        def Ezs(i, k, h, e):
            if i % 2 == 0 and k == 0 and h == 0:
                zs[i // 2] = new("zs%d" % (i // 2), [4, V], F32)
            copy(e, zs[i // 2][:, 2 * (i % 2) + k, 512 * h : 512 * (h + 1)], acc["zs", i, k, h][:])

        def store_zs(i):
            nc.sync.dma_start(out=zs_v[i // 2][:, 2 * (i % 2) : 2 * (i % 2) + 2, :], in_=zs[i // 2][:, 2 * (i % 2) : 2 * (i % 2) + 2, :])

        def T_c(m):
            i, k = divmod(m, 2)
            words = c_sb[i][:, k, :].bitcast(F32)
            for h in range(2):
                b = tp["c", m, h] = bank("tp", [4, P], 4)
                for q in range(2):
                    for u in range(2):
                        s = 256 * (2 * h + q)
                        nc.tensor.transpose(b[:, 2 * q + u, :], words[:, s + u : s + 256 : 2], ident[:])

        def E_c(m, h, e):
            if h == 0:
                tq["c", m] = new("tq", [2048], BF16, 4)
            evac(e, tp["c", m, h], tq["c", m][:, 1024 * h : 1024 * (h + 1)])

        def Q_c(m):
            cc[m] = quant("c%d" % m, tq["c", m][:], 2048)

        def WD(q, ch, j, e="S"):
            if j == 0:
                wide[q, ch] = new("wide", [4, NC], BF16, 4)
            src = wt_sb[q][:, j, NC * ch : NC * (ch + 1)].bitcast(FP8)
            if e == "S":
                nc.scalar.activation(out=wide[q, ch][:, j, :], in_=src, func=ACT.Copy, scale=scale_sb[:, q, j : j + 1])
            else:
                nc.vector.tensor_scalar(out=wide[q, ch][:, j, :], in0=src, scalar1=scale_sb[:, q, j : j + 1], scalar2=None, op0=ALU.mult)

        def WI(q, ch, e="V"):
            inter["wt", q, ch] = new("winter", [NC, 4], BF16, 4)
            copy(e, **interleave(inter["wt", q, ch][:], wide[q, ch][:]))

        def WQ(q, ch):
            wtc[q, ch] = quant("wt", flat(inter["wt", q, ch]), 4 * NC, 8)

        def XGI(g, h, e="V"):
            t = inter["xg", g, h] = new("inter", [512, 4], BF16, 3)
            copy(e, **interleave(t[:], x_sb[g][:, :, 512 * h : 512 * (h + 1)]))

        def XGQ(g, h):
            xgc[g, h] = quant("x%d" % (2 * g + h), flat(inter["xg", g, h]), 2048)

        def MZt(ch, i):
            b = acc["zt", ch, i] = bank("acc", [2, NC], 4)
            for k in range(2):
                cod, pl = cc[2 * i + k]
                for q in range(4):
                    w, wp = wtc[q, ch]
                    m = slice(q * P, (q + 1) * P)
                    nc.tensor.matmul_mx(out=b[:, k, :], lhsT=cod[:, m].bitcast(FP8X4), lhsT_scale=pl[:, m], rhs=w[:].bitcast(FP8X4), rhs_scale=wp[:], start=q == 0, stop=q == 3)

        def Ezt(ch, i, e="S"):
            g, k = divmod(i, 2)
            if k == 0:
                zt[g, ch] = new("zt", [4, NC], F32, 3)
            copy(e, zt[g, ch][:, 2 * k : 2 * k + 2, :], acc["zt", ch, i][:])

        def SUB(ch, i):
            g, k = divmod(i, 2)
            d = zs[g][:, 2 * k : 2 * k + 2, ch * NC : (ch + 1) * NC]
            nc.vector.tensor_tensor(out=d, in0=d, in1=acc["zt", ch, i][:], op=ALU.subtract)

        def store_zt(ch, g):
            nc.sync.dma_start(out=zt_v[g][:, :, ch * NC : (ch + 1) * NC], in_=zt[g, ch][:])

        def DM(ch, g):
            dI[g, ch] = new("dI", [NC, 4], BF16, 2)
            nc.vector.tensor_tensor(
                out=dI[g, ch][:].rearrange("p (c i) t -> p c t i", i=4),
                in0=zs[g][:, :, ch * NC : (ch + 1) * NC].rearrange("p t (c i) -> p c t i", i=4),
                in1=r32[:, g, :].unsqueeze(1).unsqueeze(3).to_broadcast([P, NC // 4, 4, 4]),
                op=ALU.mult,
            )

        def DQ(ch, g):
            dc[g, ch] = quant("d", flat(dI[g, ch]), 4 * NC, 4)

        def MG(ch, mp):
            b = acc["g", ch, mp] = bank("tp", [2, NC], 4)
            for k in range(2):
                mt = 2 * mp + k
                for g in range(2):
                    xcod, xpl = xgc[g, mt // 4]
                    dcod, dpl = dc[g, ch]
                    m = slice((mt % 4) * P, (mt % 4 + 1) * P)
                    nc.tensor.matmul_mx(out=b[:, k, :], lhsT=xcod[:, m].bitcast(FP8X4), lhsT_scale=xpl[:, m], rhs=dcod[:].bitcast(FP8X4), rhs_scale=dpl[:], start=g == 0, stop=g == 1)

        def EG(ch, mp, e):
            if mp % 2 == 0:
                gs[ch, mp // 2] = new("gs", [4, NC], F32, 3)
            out = gs[ch, mp // 2][:, 2 * (mp % 2) : 2 * (mp % 2) + 2, :]
            if e == "S":
                nc.scalar.activation(out=out, in_=acc["g", ch, mp][:], func=ACT.Copy, scale=1.0 / 32.0)
            else:
                nc.vector.tensor_scalar(out=out, in0=acc["g", ch, mp][:], scalar1=1.0 / 32.0, scalar2=None, op0=ALU.mult)

        def store_g(ch, hb):
            nc.sync.dma_start(out=g_v[:, 4 * hb : 4 * hb + 4, ch * NC : (ch + 1) * NC], in_=gs[ch, hb][:])

        E = "S"
        def wprep(q, ch):
            for j in range(4): WD(q, ch, j, E)
            WI(q, ch); WQ(q, ch)
        def zs_part(i):
            for h in range(2):
                for k in range(2):
                    MZs(i, k, h)
            for h in range(2):
                for k in range(2):
                    Ezs(i, k, h, E)
            store_zs(i)
        def xpart(i):
            T_x(i)
            E_x(i, 0, E); E_x(i, 1, E)
            Q_x(i)
        def cpart(m):
            T_c(m)
            E_c(m, 0, E); E_c(m, 1, E)
            Q_c(m)
        xpart(0)
        WSI(0, 0); WSI(0, 1); load_c(2)
        WSQ(0, 0); WSQ(0, 1)
        xpart(1)
        WSI(1, 0); WSI(1, 1); load_c(3)
        WSQ(1, 0); WSQ(1, 1)
        wprep(0, 0)
        zs_part(0)
        xpart(2)
        cpart(0)
        wprep(1, 0)
        zs_part(1)
        xpart(3)
        cpart(1)
        XGI(0, 0); XGI(0, 1)
        wprep(2, 0)
        zs_part(2)
        cpart(2)
        XGQ(0, 0); XGQ(0, 1)
        wprep(3, 0)
        zs_part(3)
        cpart(3)
        XGI(1, 0); XGI(1, 1)
        nc.vector.tensor_copy(out=r32[:], in_=r_sb[:])
        for ch in range(CH):
            for i in range(4):
                if ch == 0 and i < 2:
                    cpart(4 + 2 * i); cpart(5 + 2 * i)
                MZt(ch, i)
                if ch > 0: MG(ch - 1, i)
                SUB(ch, i); Ezt(ch, i, E)
                if ch > 0:
                    EG(ch - 1, i, E)
                    if i % 2: store_g(ch - 1, i // 2)
                if i % 2:
                    store_zt(ch, i // 2)
                    DM(ch, i // 2)
                    DQ(ch, i // 2)
                if ch < CH - 1: wprep(i, ch + 1)
                if ch == 0 and i == 1: XGQ(1, 0); XGQ(1, 1)
        for i in range(4):
            MG(CH - 1, i)
            EG(CH - 1, i, E)
            if i % 2: store_g(CH - 1, i // 2)
